import numpy as np
import ml_dtypes

BF16 = ml_dtypes.bfloat16


def bf(x):
    return np.asarray(x, np.float32).astype(BF16)


def f32(x):
    return np.asarray(x, np.float32)


def f64(x):
    return np.asarray(x).astype(np.float64)


def striped(idx):
    return np.concatenate([l.reshape(-1, 16).T for l in idx])


def rows(idx, k):
    return np.tile(np.repeat(idx, 16, axis=0), (k // (16 * 8), 1))


def look(tab, idx):
    return np.take_along_axis(f64(tab), rows(idx, len(tab)), axis=1)


K, S, V, N = 256, 2048, 1024, 1024


def setup_inputs():
    return {"tab": f32(np.random.standard_normal((2, K, S))), "offs": striped(np.stack([np.random.permutation(S)[:N] for _ in range(8)]))}


def reference(tab, offs):
    idx = np.stack([g.T.reshape(-1) for g in np.split(offs, 8)])
    x = ((look(tab[0], idx) - 0.125) * 1.5) * (np.maximum(look(tab[1], idx), 0.0))
    return x

@@ -1,0 +1,46 @@
+import concourse.mybir as mybir
+
+P = 128
+GROUP = 16
+PIECE = 512
+SHIFT, SCALE = 0.125, 1.5
+
+F32, U16 = mybir.dt.float32, mybir.dt.uint16
+ALU = mybir.AluOpType
+RELU = mybir.ActivationFunctionType.Relu
+
+
+def tile_lookup_vg_nrmrelu_out_kernel(tc, tab, offs, out):
+    nc = tc.nc
+    rows, places = tab.shape[1], tab.shape[2]
+    entries = out.shape[1]
+    blocks, pieces = rows // P, entries // PIECE
+    cols = PIECE // GROUP
+
+    with (
+        tc.tile_pool(name="held", bufs=1) as held,
+        tc.tile_pool(name="work", bufs=blocks * pieces) as work,
+    ):
+        offsets = held.tile([P, entries // GROUP], U16, name="offsets")
+        nc.sync.dma_start(offsets[:], offs)
+
+        values, gates = [], []
+        for b in range(blocks):
+            values.append(held.tile([P, places], F32, name=f"values{b}"))
+            gates.append(held.tile([P, places], F32, name=f"gates{b}"))
+            nc.sync.dma_start(values[b][:], tab[0, b * P : (b + 1) * P, :])
+            nc.sync.dma_start(gates[b][:], tab[1, b * P : (b + 1) * P, :])
+
+        for b in range(blocks):
+            scaled = []
+            for k in range(pieces):
+                scaled.append(work.tile([P, PIECE], F32, name="scaled"))
+                picked = values[b][:].indirect(offsets[:, k * cols : (k + 1) * cols])
+                nc.vector.tensor_scalar(scaled[k][:], picked, SHIFT, SCALE, ALU.subtract, ALU.mult)
+            for k in range(pieces):
+                opened = work.tile([P, PIECE], F32, name="opened")
+                picked = gates[b][:].indirect(offsets[:, k * cols : (k + 1) * cols])
+                nc.scalar.activation(opened[:], picked, RELU)
+                product = work.tile([P, PIECE], F32, name="product")
+                nc.vector.tensor_tensor(product[:], scaled[k][:], opened[:], ALU.mult)
+                nc.sync.dma_start(out[b * P : (b + 1) * P, k * PIECE : (k + 1) * PIECE], product[:])

@@ -24,6 +24,11 @@ def tile_lookup_vg_nrmrelu_out_kernel(tc, tab, offs, out):
         offsets = held.tile([P, entries // GROUP], U16, name="offsets")
         nc.sync.dma_start(offsets[:], offs)
 
+        warm_in = held.tile([P, 8], F32, name="warm_in")
+        warm_out = held.tile([P, 8], F32, name="warm_out")
+        nc.vector.memset(warm_in[:], 0.0)
+        nc.scalar.activation(warm_out[:], warm_in[:], RELU)
+
         values, gates = [], []
         for b in range(blocks):
             values.append(held.tile([P, places], F32, name=f"values{b}"))
@@ -41,6 +46,11 @@ def tile_lookup_vg_nrmrelu_out_kernel(tc, tab, offs, out):
                 opened = work.tile([P, PIECE], F32, name="opened")
                 picked = gates[b][:].indirect(offsets[:, k * cols : (k + 1) * cols])
                 nc.scalar.activation(opened[:], picked, RELU)
-                product = work.tile([P, PIECE], F32, name="product")
-                nc.vector.tensor_tensor(product[:], scaled[k][:], opened[:], ALU.mult)
-                nc.sync.dma_start(out[b * P : (b + 1) * P, k * PIECE : (k + 1) * PIECE], product[:])
+                parts = 2 if (b, k) == (blocks - 1, pieces - 1) else 1
+                width = PIECE // parts
+                for h in range(parts):
+                    product = work.tile([P, width], F32, name=f"product{parts}")
+                    part = slice(h * width, (h + 1) * width)
+                    nc.vector.tensor_tensor(product[:], scaled[k][:, part], opened[:, part], ALU.mult)
+                    first = k * PIECE + h * width
+                    nc.sync.dma_start(out[b * P : (b + 1) * P, first : first + width], product[:])

@@ -24,17 +24,18 @@ def tile_lookup_vg_nrmrelu_out_kernel(tc, tab, offs, out):
         offsets = held.tile([P, entries // GROUP], U16, name="offsets")
         nc.sync.dma_start(offsets[:], offs)
 
-        warm_in = held.tile([P, 8], F32, name="warm_in")
-        warm_out = held.tile([P, 8], F32, name="warm_out")
-        nc.vector.memset(warm_in[:], 0.0)
-        nc.scalar.activation(warm_out[:], warm_in[:], RELU)
-
         values, gates = [], []
         for b in range(blocks):
             values.append(held.tile([P, places], F32, name=f"values{b}"))
             gates.append(held.tile([P, places], F32, name=f"gates{b}"))
-            nc.sync.dma_start(values[b][:], tab[0, b * P : (b + 1) * P, :])
+            queue = nc.scalar if b == 0 else nc.sync
+            queue.dma_start(values[b][:], tab[0, b * P : (b + 1) * P, :])
             nc.sync.dma_start(gates[b][:], tab[1, b * P : (b + 1) * P, :])
+
+        warm_in = held.tile([P, 8], F32, name="warm_in")
+        warm_out = held.tile([P, 8], F32, name="warm_out")
+        nc.vector.memset(warm_in[:], 0.0)
+        nc.scalar.activation(warm_out[:], warm_in[:], RELU)
 
         for b in range(blocks):
             scaled = []

@@ -47,11 +47,10 @@ def tile_lookup_vg_nrmrelu_out_kernel(tc, tab, offs, out):
                 opened = work.tile([P, PIECE], F32, name="opened")
                 picked = gates[b][:].indirect(offsets[:, k * cols : (k + 1) * cols])
                 nc.scalar.activation(opened[:], picked, RELU)
-                parts = 2 if (b, k) == (blocks - 1, pieces - 1) else 1
-                width = PIECE // parts
-                for h in range(parts):
-                    product = work.tile([P, width], F32, name=f"product{parts}")
-                    part = slice(h * width, (h + 1) * width)
-                    nc.vector.tensor_tensor(product[:], scaled[k][:, part], opened[:, part], ALU.mult)
-                    first = k * PIECE + h * width
-                    nc.sync.dma_start(out[b * P : (b + 1) * P, first : first + width], product[:])
+                last = (b, k) == (blocks - 1, pieces - 1)
+                cuts = (0, 3 * PIECE // 4, PIECE) if last else (0, PIECE)
+                for lo, hi in zip(cuts, cuts[1:]):
+                    product = work.tile([P, hi - lo], F32, name=f"product{hi - lo}")
+                    nc.vector.tensor_tensor(product[:], scaled[k][:, lo:hi], opened[:, lo:hi], ALU.mult)
+                    queue = nc.scalar if last and hi == PIECE else nc.sync
+                    queue.dma_start(out[b * P : (b + 1) * P, k * PIECE + lo : k * PIECE + hi], product[:])

import concourse.mybir as mybir

P = 128
GROUP = 16
PIECE = 512
SHIFT, SCALE = 0.125, 1.5

F32, U16 = mybir.dt.float32, mybir.dt.uint16
ALU = mybir.AluOpType
RELU = mybir.ActivationFunctionType.Relu


def tile_lookup_vg_nrmrelu_out_kernel(tc, tab, offs, out):
    nc = tc.nc
    rows, places = tab.shape[1], tab.shape[2]
    entries = out.shape[1]
    blocks, pieces = rows // P, entries // PIECE
    cols = PIECE // GROUP

    with (
        tc.tile_pool(name="held", bufs=1) as held,
        tc.tile_pool(name="work", bufs=blocks * pieces) as work,
    ):
        offsets = held.tile([P, entries // GROUP], U16, name="offsets")
        nc.sync.dma_start(offsets[:], offs)

        values, gates = [], []
        for b in range(blocks):
            values.append(held.tile([P, places], F32, name=f"values{b}"))
            gates.append(held.tile([P, places], F32, name=f"gates{b}"))
            queue = nc.scalar if b == 0 else nc.sync
            queue.dma_start(values[b][:], tab[0, b * P : (b + 1) * P, :])
            nc.sync.dma_start(gates[b][:], tab[1, b * P : (b + 1) * P, :])

        warm_in = held.tile([P, 8], F32, name="warm_in")
        warm_out = held.tile([P, 8], F32, name="warm_out")
        nc.vector.memset(warm_in[:], 0.0)
        nc.scalar.activation(warm_out[:], warm_in[:], RELU)

        for b in range(blocks):
            scaled = []
            for k in range(pieces):
                scaled.append(work.tile([P, PIECE], F32, name="scaled"))
                picked = values[b][:].indirect(offsets[:, k * cols : (k + 1) * cols])
                nc.vector.tensor_scalar(scaled[k][:], picked, SHIFT, SCALE, ALU.subtract, ALU.mult)
            for k in range(pieces):
                opened = work.tile([P, PIECE], F32, name="opened")
                picked = gates[b][:].indirect(offsets[:, k * cols : (k + 1) * cols])
                nc.scalar.activation(opened[:], picked, RELU)
                last = (b, k) == (blocks - 1, pieces - 1)
                cuts = (0, 3 * PIECE // 4, PIECE) if last else (0, PIECE)
                for lo, hi in zip(cuts, cuts[1:]):
                    product = work.tile([P, hi - lo], F32, name=f"product{hi - lo}")
                    nc.vector.tensor_tensor(product[:], scaled[k][:, lo:hi], opened[:, lo:hi], ALU.mult)
                    queue = nc.scalar if last and hi == PIECE else nc.sync
                    queue.dma_start(out[b * P : (b + 1) * P, k * PIECE + lo : k * PIECE + hi], product[:])
